import numpy as np, ml_dtypes
CORES = [2,3,42,43,82,83,122,123]
N = 8
import mx_ref
NC, G = 256, 4
C = np.float32(0.041)
BF = ml_dtypes.bfloat16
def cut(t, i, w=512):
    return t[:, w * i:w * i + w]
def tile(rs):
    return np.stack(rs, axis=2).reshape(128, -1).astype(BF)
def layer(w, X):
    out = []
    for i in range(G):
        for t in range(len(X)):
            p = mx_ref.matmul(mx_ref.quantize(cut(w, len(X) * i + t)), X[t])
            z = p if t == 0 else z + p
        out.append(z)
    return out
def masked(A, E):
    return [(e * (a > 0)) * C for a, e in zip(A, E)]
def setup_inputs(rng):
    def f(*shape):
        return mx_ref.flush((rng.standard_normal(shape, dtype=np.float32) * np.exp2(rng.integers(-2, 3, shape[:-1] + (1,)))).astype(BF))
    return {"x": f(N, 128, 512), "e": f(N, 128, 512), "a": f(N, 128, G * 512), "w": f(N, 128, 512), "v": f(N, 128, 4 * NC)}
def setup_inputs_blocks(rng):
    d = setup_inputs(rng)
    for k in ("x", "e", "a", "w", "v"): d[k] = mx_ref.spread(d[k], rng, 2)
    return d
def setup_inputs_wide(rng):
    d = setup_inputs(rng)
    for k in ("x", "e", "a", "w", "v"): d[k] = mx_ref.flush((d[k].astype(np.float32) * np.exp2(rng.integers(-6, 7, (N, 1, 1))).astype(np.float32)).astype(BF))
    return d
def setup_inputs_zeros(rng):
    d = setup_inputs(rng); v = d["x"].reshape(N, 128, -1, 4).copy()
    v[np.broadcast_to((rng.random((N, 1, v.shape[2], 1)) < 0.33), v.shape)] = 0
    d["x"] = v.reshape(d["x"].shape)
    return d
def reference(x, e, a, w, v):
    T = [mx_ref.quantize(tile(masked(layer(a[j], [mx_ref.quantize(x[j])]), layer(a[j], [mx_ref.quantize(e[j])])))) for j in range(N)]
    y = np.zeros((N, 128, N * 128), np.float32); z = np.zeros((N, 128, NC), np.float32)
    for r in range(N):
        qw = mx_ref.quantize(w[r]); qv = mx_ref.quantize(v[r])
        for j in range(N):
            y[r][:, 128 * j:128 * j + 128] = mx_ref.matmul(qw, T[j])
            p = mx_ref.matmul(T[j], qv)
            z[r] = p if j == 0 else z[r] + p
    return {"y": y, "z": z}

@@ -1,0 +1,202 @@
+from concourse.bass import DstId, RemoteDMATransfer
+from concourse.mybir import dt, AluOpType, ActivationFunctionType
+
+N = 8
+G = 4
+L = 128
+C = 0.041
+
+SCRATCH = {
+    "xe": ("sbuf", [128, 8 * L], "bfloat16"), "qxe": ("sbuf", [128, 2 * L], "float8_e4m3fn_x4"), "sxe": ("sbuf", [128, 2 * L], "uint8"),
+    "ab": ("sbuf", [128, 16 * L], "bfloat16"), "qa": ("sbuf", [128, 4 * L], "float8_e4m3fn_x4"), "sa": ("sbuf", [128, 4 * L], "uint8"),
+    "wb": ("sbuf", [128, 4 * L], "bfloat16"), "qw": ("sbuf", [128, L], "float8_e4m3fn_x4"), "sw": ("sbuf", [128, L], "uint8"),
+    "vb": ("sbuf", [128, 8 * L], "bfloat16"), "qv": ("sbuf", [128, 2 * L], "float8_e4m3fn_x4"), "sv": ("sbuf", [128, 2 * L], "uint8"),
+    "m": ("sbuf", [128, 4 * L], "float32"), "t": ("sbuf", [128, 4 * L], "bfloat16"),
+    "q": ("sbuf", [128, N * L], "float8_e4m3fn_x4"), "s": ("sbuf", [128, N * L], "uint8"),
+    "ysb": ("sbuf", [128, N * L], "float32"), "zsb": ("sbuf", [128, 2 * L], "float32"),
+}
+for _k in range(8):
+    SCRATCH["p%d" % _k] = ("psum", [128, 512], "float32")
+
+SEMAPHORES = (["ld_xe", "ld_a0", "ld_a1", "ld_w", "ld_v", "q_xe", "q_w", "q_v", "q_t",
+               "off_c", "off_s", "peer", "fwd", "sent", "y_pair", "y_dir", "z_all", "c_pair", "c_dir", "c_z", "st"]
+              + ["%s%d" % (n, b) for n in ("q_a", "u", "d", "mk", "tt") for b in range(G)]
+              + ["%s%d" % (n, b) for n in ("y_fwd", "c_fwd") for b in range(3)])
+
+
+def bits(mask):
+    return bin(mask).count("1")
+
+
+def rank_program(g, core, T, topo):
+    rank = T.rank_of(core)
+    if rank is None:
+        return
+    S = T.sem
+    V, P, A, Y = g.vector, g.tensor, g.scalar, g.sync
+
+    chips = []
+    for c in T.cores:
+        if topo.chip(c) not in chips:
+            chips.append(topo.chip(c))
+    ranks = [[r for r, c in enumerate(T.cores) if topo.chip(c) == ch] for ch in chips]
+    order = [r for rs in ranks for r in rs]
+    my = chips.index(topo.chip(core))
+    per = len(ranks[my])
+
+    def slot_on(d, r):
+        return (order.index(r) - per * d) % N
+
+    def rank_in(k):
+        return order[(k + per * my) % N]
+
+    own = slot_on(my, rank)
+    mate = 1 - own
+    peer = T.cores[rank_in(mate)]
+    runs = ((2, 5), (5, 8))
+    mine, theirs = runs[own], runs[mate]
+
+    def cols(k, n=1, w=L):
+        return slice(k * w, (k + n) * w)
+
+    def codes(k, n=1):
+        return T.q[:, cols(k, n)].bitcast(dt.uint8)
+
+    def plane(k, n=1):
+        return T.s[:, cols(k, n)]
+
+    def did(c):
+        rid, pid, _ = topo.addr(c)
+        return DstId(rid=rid, pnc=pid)
+
+    Y.dma_start(T.xe[:, 0:4 * L], T.x[:]).then_inc(S["ld_xe"], 16)
+    A.dma_start(T.xe[:, 4 * L:8 * L], T.e[:]).then_inc(S["ld_xe"], 16)
+    Y.dma_start(T.ab[:, 0:8 * L], T.a[:, 0:8 * L]).then_inc(S["ld_a0"], 16)
+    Y.dma_start(T.ab[:, 8 * L:16 * L], T.a[:, 8 * L:16 * L]).then_inc(S["ld_a1"], 16)
+    Y.wait_ge(S["ld_xe"], 32)
+    Y.dma_start(T.wb[:], T.w[:]).then_inc(S["ld_w"], 16)
+    Y.dma_start(T.vb[:], T.v[:]).then_inc(S["ld_v"], 16)
+
+    V.wait_ge(S["ld_xe"], 32)
+    V.quantize_mx(T.qxe[:], T.sxe[:], T.xe[:]).then_inc(S["q_xe"], 1)
+    for h in range(2):
+        V.wait_ge(S["ld_a%d" % h], 16)
+        for b in (2 * h, 2 * h + 1):
+            V.quantize_mx(T.qa[:, cols(b)], T.sa[:, cols(b)], T.ab[:, cols(b, 1, 4 * L)]).then_inc(S["q_a%d" % b], 1)
+        for b in (2 * h, 2 * h + 1):
+            V.wait_ge(S["u%d" % b], 1)
+            V.tensor_scalar(T.m[:, cols(b)], T["p%d" % b][:, 0:L], 0.0, C, AluOpType.is_gt, AluOpType.mult).then_inc(S["mk%d" % b], 1)
+        for b in (2 * h, 2 * h + 1):
+            V.wait_ge(S["d%d" % b], 1)
+            V.wait_ge(S["mk%d" % b], 1)
+            V.tensor_tensor(T.t[:, b:4 * L:4], T["p%d" % (4 + b)][:, 0:L], T.m[:, cols(b)], AluOpType.mult).then_inc(S["tt%d" % b], 1)
+    for b in range(G):
+        V.wait_ge(S["tt%d" % b], 1)
+    V.quantize_mx(T.q[:, cols(own)], T.s[:, cols(own)], T.t[:]).then_inc(S["q_t"], 1)
+    V.wait_ge(S["ld_v"], 16)
+    V.quantize_mx(T.qv[:], T.sv[:], T.vb[:]).then_inc(S["q_v"], 1)
+    V.wait_ge(S["ld_w"], 16)
+    V.quantize_mx(T.qw[:], T.sw[:], T.wb[:]).then_inc(S["q_w"], 1)
+
+    def first(b, k):
+        P.matmul_mx(T["p%d" % (4 * k + b)][:, 0:L], T.qa[:, cols(b)], T.sa[:, cols(b)],
+                    T.qxe[:, cols(k)], T.sxe[:, cols(k)], True, True).then_inc(S["%s%d" % ("ud"[k], b)], 1)
+
+    P.wait_ge(S["q_xe"], 1)
+    for h in range(2):
+        for b in (2 * h, 2 * h + 1):
+            P.wait_ge(S["q_a%d" % b], 1)
+            first(b, 0)
+        for b in (2 * h, 2 * h + 1):
+            first(b, 1)
+
+    dst = []
+    for k in range(1, len(chips)):
+        d = (my + k) % len(chips)
+        sl = slot_on(d, rank)
+        to = ranks[d][[i for i, (lo, hi) in enumerate(runs) if lo <= sl < hi][0]]
+        dst.append((T.cores[to], sl))
+    far = topo.mask(core, dst[0][0])
+    for c, _ in dst:
+        far &= topo.mask(core, c)
+    near = topo.mask(core, peer)
+    side = near & ~far
+    sent = [0]
+
+    def send(to, view, slots, n, src, mask, sem):
+        g.remote_dma_fused([RemoteDMATransfer(dst_ids=[did(c) for c in to], dma_engine_mask=mask, remote_sem=S[sem],
+                                              src=view(src, n), dsts=[view(k, n) for k in slots])], local_sem=S["sent"])
+        sent[0] += bits(mask)
+
+    g.wait_ge(S["q_t"], 1)
+    for view, sem in ((codes, "off_c"), (plane, "off_s")):
+        send([c for c, _ in dst], view, [k for _, k in dst], 1, own, far, sem)
+    for view in (codes, plane):
+        send([peer], view, [own], 1, own, side, "peer")
+    got = 3 * bits(far)
+    for view, sem in ((codes, "off_c"), (plane, "off_s")):
+        g.wait_ge(S[sem], got)
+        send([peer], view, [mine[0]], 3, mine[0], near, "fwd")
+    g.wait_ge(S["sent"], sent[0])
+
+    def zed(k, start, stop):
+        return P.matmul_mx(T.p0[:, 0:2 * L], T.q[:, cols(k)], T.s[:, cols(k)], T.qv[:], T.sv[:], start, stop)
+
+    def why(bank, k, n):
+        return P.matmul_mx(T["p%d" % bank][:, 0:n * L], T.qw[:], T.sw[:], T.q[:, cols(k, n)], T.s[:, cols(k, n)], True, True)
+
+    P.wait_ge(S["q_t"], 1)
+    P.wait_ge(S["q_v"], 1)
+    zed(own, True, False)
+    P.wait_ge(S["q_w"], 1)
+    P.wait_ge(S["peer"], 2 * bits(side))
+    why(1, 0, 2).then_inc(S["y_pair"], 1)
+    zed(mate, False, False)
+    P.wait_ge(S["off_c"], got)
+    P.wait_ge(S["off_s"], got)
+    why(2, mine[0], 3).then_inc(S["y_dir"], 1)
+    for k in range(*mine):
+        zed(k, False, False)
+    P.wait_ge(S["fwd"], 2 * bits(near))
+    for i in range(3):
+        why(3 + i, theirs[0] + i, 1).then_inc(S["y_fwd%d" % i], 1)
+    for k in range(*theirs):
+        last = zed(k, False, k == theirs[1] - 1)
+    last.then_inc(S["z_all"], 1)
+
+    def act(bank, k, n, wait, done):
+        A.wait_ge(S[wait], 1)
+        A.activation(T.ysb[:, cols(k, n)], T["p%d" % bank][:, 0:n * L], ActivationFunctionType.Copy).then_inc(S[done], 1)
+
+    act(1, 0, 2, "y_pair", "c_pair")
+    act(2, mine[0], 3, "y_dir", "c_dir")
+    act(3, theirs[0], 1, "y_fwd0", "c_fwd0")
+    V.wait_ge(S["y_fwd1"], 1)
+    V.tensor_copy(T.ysb[:, cols(theirs[0] + 1)], T.p4[:, 0:L]).then_inc(S["c_fwd1"], 1)
+    act(5, theirs[0] + 2, 1, "y_fwd2", "c_fwd2")
+    V.wait_ge(S["z_all"], 1)
+    V.tensor_copy(T.zsb[:], T.p0[:, 0:2 * L]).then_inc(S["c_z"], 1)
+
+    stored = [0]
+
+    def store(lo, hi):
+        k = lo
+        while k < hi:
+            n = 1
+            while k + n < hi and rank_in(k + n) == rank_in(k) + n:
+                n += 1
+            Y.dma_start(T.y[:, cols(rank_in(k), n)], T.ysb[:, cols(k, n)]).then_inc(S["st"], 16)
+            stored[0] += 16
+            k += n
+
+    Y.wait_ge(S["c_pair"], 1)
+    store(0, 2)
+    Y.wait_ge(S["c_dir"], 1)
+    store(*mine)
+    for i in range(3):
+        Y.wait_ge(S["c_fwd%d" % i], 1)
+    store(*theirs)
+    A.wait_ge(S["c_z"], 1)
+    A.dma_start(T.z[:], T.zsb[:]).then_inc(S["st"], 16)
+    stored[0] += 16
+    Y.wait_ge(S["st"], stored[0])

@@ -5,23 +5,25 @@ N = 8
 G = 4
 L = 128
 C = 0.041
+FAR = (1, 2, 3)
+S_MASK = (0, 1)
 
 SCRATCH = {
-    "xe": ("sbuf", [128, 8 * L], "bfloat16"), "qxe": ("sbuf", [128, 2 * L], "float8_e4m3fn_x4"), "sxe": ("sbuf", [128, 2 * L], "uint8"),
+    "xb": ("sbuf", [128, 4 * L], "bfloat16"), "eb": ("sbuf", [128, 4 * L], "bfloat16"),
+    "qxe": ("sbuf", [128, 2 * L], "float8_e4m3fn_x4"), "sxe": ("sbuf", [128, 2 * L], "uint8"),
     "ab": ("sbuf", [128, 16 * L], "bfloat16"), "qa": ("sbuf", [128, 4 * L], "float8_e4m3fn_x4"), "sa": ("sbuf", [128, 4 * L], "uint8"),
     "wb": ("sbuf", [128, 4 * L], "bfloat16"), "qw": ("sbuf", [128, L], "float8_e4m3fn_x4"), "sw": ("sbuf", [128, L], "uint8"),
     "vb": ("sbuf", [128, 8 * L], "bfloat16"), "qv": ("sbuf", [128, 2 * L], "float8_e4m3fn_x4"), "sv": ("sbuf", [128, 2 * L], "uint8"),
-    "m": ("sbuf", [128, 4 * L], "float32"), "t": ("sbuf", [128, 4 * L], "bfloat16"),
+    "sg": ("sbuf", [128, 4 * L], "float32"), "m": ("sbuf", [128, 4 * L], "float32"), "t": ("sbuf", [128, 4 * L], "bfloat16"),
     "q": ("sbuf", [128, N * L], "float8_e4m3fn_x4"), "s": ("sbuf", [128, N * L], "uint8"),
     "ysb": ("sbuf", [128, N * L], "float32"), "zsb": ("sbuf", [128, 2 * L], "float32"),
 }
 for _k in range(8):
     SCRATCH["p%d" % _k] = ("psum", [128, 512], "float32")
 
-SEMAPHORES = (["ld_xe", "ld_a0", "ld_a1", "ld_w", "ld_v", "q_xe", "q_w", "q_v", "q_t",
-               "off_c", "off_s", "peer", "fwd", "sent", "y_pair", "y_dir", "z_all", "c_pair", "c_dir", "c_z", "st"]
-              + ["%s%d" % (n, b) for n in ("q_a", "u", "d", "mk", "tt") for b in range(G)]
-              + ["%s%d" % (n, b) for n in ("y_fwd", "c_fwd") for b in range(3)])
+SEMAPHORES = (["ld_x", "ld_e", "ld_w", "ld_v", "q_x", "q_e", "q_w", "q_v", "q_t", "peer", "sent", "z_all", "c_z", "y_p", "c_p", "st"]
+              + ["%s%d" % (n, b) for n in ("ld_a", "q_a", "u", "d", "sg", "mk", "tt") for b in range(G)]
+              + ["%s%d" % (n, k) for n in ("dc", "dp", "f", "y_d", "y_f", "c_d", "c_f") for k in FAR])
 
 
 def bits(mask):
@@ -40,104 +42,110 @@ def rank_program(g, core, T, topo):
         if topo.chip(c) not in chips:
             chips.append(topo.chip(c))
     ranks = [[r for r, c in enumerate(T.cores) if topo.chip(c) == ch] for ch in chips]
-    order = [r for rs in ranks for r in rs]
     my = chips.index(topo.chip(core))
-    per = len(ranks[my])
+    i = ranks[my].index(rank)
+    mate = ranks[my][1 - i]
+    peer = T.cores[mate]
 
-    def slot_on(d, r):
-        return (order.index(r) - per * d) % N
-
-    def rank_in(k):
-        return order[(k + per * my) % N]
-
-    own = slot_on(my, rank)
-    mate = 1 - own
-    peer = T.cores[rank_in(mate)]
-    runs = ((2, 5), (5, 8))
-    mine, theirs = runs[own], runs[mate]
+    def came(kind, k):
+        return ranks[(my - k) % len(chips)][i if kind == "d" else 1 - i]
 
     def cols(k, n=1, w=L):
         return slice(k * w, (k + n) * w)
 
-    def codes(k, n=1):
-        return T.q[:, cols(k, n)].bitcast(dt.uint8)
+    def codes(k):
+        return T.q[:, cols(k)].bitcast(dt.uint8)
 
-    def plane(k, n=1):
-        return T.s[:, cols(k, n)]
+    def plane(k):
+        return T.s[:, cols(k)]
 
-    def did(c):
-        rid, pid, _ = topo.addr(c)
-        return DstId(rid=rid, pnc=pid)
+    def load_a(b, queue):
+        queue.dma_start(T.ab[:, cols(b, 1, 4 * L)], T.a[:, cols(b, 1, 4 * L)]).then_inc(S["ld_a%d" % b], 16)
 
-    Y.dma_start(T.xe[:, 0:4 * L], T.x[:]).then_inc(S["ld_xe"], 16)
-    A.dma_start(T.xe[:, 4 * L:8 * L], T.e[:]).then_inc(S["ld_xe"], 16)
-    Y.dma_start(T.ab[:, 0:8 * L], T.a[:, 0:8 * L]).then_inc(S["ld_a0"], 16)
-    Y.dma_start(T.ab[:, 8 * L:16 * L], T.a[:, 8 * L:16 * L]).then_inc(S["ld_a1"], 16)
-    Y.wait_ge(S["ld_xe"], 32)
-    Y.dma_start(T.wb[:], T.w[:]).then_inc(S["ld_w"], 16)
+    Y.dma_start(T.xb[:], T.x[:]).then_inc(S["ld_x"], 16)
+    load_a(0, A)
+    Y.dma_start(T.eb[:], T.e[:]).then_inc(S["ld_e"], 16)
+    for b in (1, 2, 3):
+        load_a(b, Y)
+    Y.wait_ge(S["ld_x"], 16)
+    Y.wait_ge(S["ld_e"], 16)
     Y.dma_start(T.vb[:], T.v[:]).then_inc(S["ld_v"], 16)
+    Y.dma_start(T.wb[:], T.w[:]).then_inc(S["ld_w"], 16)
 
-    V.wait_ge(S["ld_xe"], 32)
-    V.quantize_mx(T.qxe[:], T.sxe[:], T.xe[:]).then_inc(S["q_xe"], 1)
-    for h in range(2):
-        V.wait_ge(S["ld_a%d" % h], 16)
-        for b in (2 * h, 2 * h + 1):
-            V.quantize_mx(T.qa[:, cols(b)], T.sa[:, cols(b)], T.ab[:, cols(b, 1, 4 * L)]).then_inc(S["q_a%d" % b], 1)
-        for b in (2 * h, 2 * h + 1):
-            V.wait_ge(S["u%d" % b], 1)
-            V.tensor_scalar(T.m[:, cols(b)], T["p%d" % b][:, 0:L], 0.0, C, AluOpType.is_gt, AluOpType.mult).then_inc(S["mk%d" % b], 1)
-        for b in (2 * h, 2 * h + 1):
-            V.wait_ge(S["d%d" % b], 1)
-            V.wait_ge(S["mk%d" % b], 1)
-            V.tensor_tensor(T.t[:, b:4 * L:4], T["p%d" % (4 + b)][:, 0:L], T.m[:, cols(b)], AluOpType.mult).then_inc(S["tt%d" % b], 1)
+    def q_in(k):
+        nm = "xe"[k]
+        V.wait_ge(S["ld_" + nm], 16)
+        V.quantize_mx(T.qxe[:, cols(k)], T.sxe[:, cols(k)], T[nm + "b"][:]).then_inc(S["q_" + nm], 1)
+
+    def q_a(b):
+        V.wait_ge(S["ld_a%d" % b], 16)
+        V.quantize_mx(T.qa[:, cols(b)], T.sa[:, cols(b)], T.ab[:, cols(b, 1, 4 * L)]).then_inc(S["q_a%d" % b], 1)
+
+    def mask(b):
+        V.wait_ge(S["u%d" % b], 1)
+        V.tensor_scalar(T.m[:, cols(b)], T["p%d" % b][:, 0:L], 0.0, C, AluOpType.is_gt, AluOpType.mult).then_inc(S["mk%d" % b], 1)
+
+    def piece(b):
+        V.wait_ge(S["d%d" % b], 1)
+        V.wait_ge(S["mk%d" % b], 1)
+        V.tensor_tensor(T.t[:, b:4 * L:4], T["p%d" % (4 + b)][:, 0:L], T.m[:, cols(b)], AluOpType.mult).then_inc(S["tt%d" % b], 1)
+
+    for call, b in ((q_in, 0), (q_a, 0), (q_in, 1), (q_a, 1), (piece, 0), (q_a, 2), (q_a, 3), (piece, 1),
+                    (mask, 2), (mask, 3), (piece, 2), (piece, 3)):
+        call(b)
     for b in range(G):
         V.wait_ge(S["tt%d" % b], 1)
-    V.quantize_mx(T.q[:, cols(own)], T.s[:, cols(own)], T.t[:]).then_inc(S["q_t"], 1)
+    V.quantize_mx(T.q[:, cols(rank)], T.s[:, cols(rank)], T.t[:]).then_inc(S["q_t"], 1)
     V.wait_ge(S["ld_v"], 16)
     V.quantize_mx(T.qv[:], T.sv[:], T.vb[:]).then_inc(S["q_v"], 1)
     V.wait_ge(S["ld_w"], 16)
     V.quantize_mx(T.qw[:], T.sw[:], T.wb[:]).then_inc(S["q_w"], 1)
 
-    def first(b, k):
-        P.matmul_mx(T["p%d" % (4 * k + b)][:, 0:L], T.qa[:, cols(b)], T.sa[:, cols(b)],
-                    T.qxe[:, cols(k)], T.sxe[:, cols(k)], True, True).then_inc(S["%s%d" % ("ud"[k], b)], 1)
+    for b in S_MASK:
+        A.wait_ge(S["u%d" % b], 1)
+        A.activation(T.sg[:, cols(b)], T["p%d" % b][:, 0:L], ActivationFunctionType.Sign).then_inc(S["sg%d" % b], 1)
+        A.wait_ge(S["sg%d" % b], 1)
+        A.activation(T.m[:, cols(b)], T.sg[:, cols(b)], ActivationFunctionType.Relu, scale=C).then_inc(S["mk%d" % b], 1)
 
-    P.wait_ge(S["q_xe"], 1)
-    for h in range(2):
-        for b in (2 * h, 2 * h + 1):
+    for b in range(G):
+        for k in range(2):
+            P.wait_ge(S["q_" + "xe"[k]], 1)
             P.wait_ge(S["q_a%d" % b], 1)
-            first(b, 0)
-        for b in (2 * h, 2 * h + 1):
-            first(b, 1)
+            P.matmul_mx(T["p%d" % (4 * k + b)][:, 0:L], T.qa[:, cols(b)], T.sa[:, cols(b)],
+                        T.qxe[:, cols(k)], T.sxe[:, cols(k)], True, True).then_inc(S["%s%d" % ("ud"[k], b)], 1)
 
-    dst = []
-    for k in range(1, len(chips)):
-        d = (my + k) % len(chips)
-        sl = slot_on(d, rank)
-        to = ranks[d][[i for i, (lo, hi) in enumerate(runs) if lo <= sl < hi][0]]
-        dst.append((T.cores[to], sl))
-    far = topo.mask(core, dst[0][0])
-    for c, _ in dst:
-        far &= topo.mask(core, c)
+    to = {k: T.cores[ranks[(my + k) % len(chips)][i]] for k in FAR}
     near = topo.mask(core, peer)
+    far = near
+    for k in FAR:
+        far &= topo.mask(core, to[k])
     side = near & ~far
+    nf, ns = bits(far), bits(side)
     sent = [0]
 
-    def send(to, view, slots, n, src, mask, sem):
-        g.remote_dma_fused([RemoteDMATransfer(dst_ids=[did(c) for c in to], dma_engine_mask=mask, remote_sem=S[sem],
-                                              src=view(src, n), dsts=[view(k, n) for k in slots])], local_sem=S["sent"])
+    def part(dst, view, slot, mask, sem):
+        rid, pid, _ = topo.addr(dst)
         sent[0] += bits(mask)
+        return RemoteDMATransfer(dst_ids=[DstId(rid=rid, pnc=pid)], dma_engine_mask=mask, remote_sem=S[sem],
+                                 src=view(slot), dsts=[view(slot)])
 
+    both = (("dc", codes), ("dp", plane))
     g.wait_ge(S["q_t"], 1)
-    for view, sem in ((codes, "off_c"), (plane, "off_s")):
-        send([c for c, _ in dst], view, [k for _, k in dst], 1, own, far, sem)
-    for view in (codes, plane):
-        send([peer], view, [own], 1, own, side, "peer")
-    got = 3 * bits(far)
-    for view, sem in ((codes, "off_c"), (plane, "off_s")):
-        g.wait_ge(S[sem], got)
-        send([peer], view, [mine[0]], 3, mine[0], near, "fwd")
+    for k in FAR:
+        for sem, view in both:
+            parts = [part(to[k], view, rank, far, "%s%d" % (sem, k))]
+            if k == FAR[1]:
+                parts.append(part(peer, view, rank, side, "peer"))
+            g.remote_dma_fused(parts, local_sem=S["sent"])
+    via = {k: side for k in FAR}
+    via[FAR[-1]] = near
+    for k in FAR:
+        for sem, view in both:
+            g.wait_ge(S["%s%d" % (sem, k)], nf)
+            g.remote_dma_fused([part(peer, view, came("d", k), via[k], "f%d" % k)], local_sem=S["sent"])
     g.wait_ge(S["sent"], sent[0])
+
+    seq = [("d", FAR[0]), ("d", FAR[1]), ("f", FAR[0]), ("d", FAR[2]), ("f", FAR[1]), ("f", FAR[2])]
 
     def zed(k, start, stop):
         return P.matmul_mx(T.p0[:, 0:2 * L], T.q[:, cols(k)], T.s[:, cols(k)], T.qv[:], T.sv[:], start, stop)
@@ -147,56 +155,55 @@ def rank_program(g, core, T, topo):
 
     P.wait_ge(S["q_t"], 1)
     P.wait_ge(S["q_v"], 1)
-    zed(own, True, False)
+    zed(rank, True, False)
     P.wait_ge(S["q_w"], 1)
-    P.wait_ge(S["peer"], 2 * bits(side))
-    why(1, 0, 2).then_inc(S["y_pair"], 1)
+    P.wait_ge(S["peer"], 2 * ns)
+    why(1, min(rank, mate), 2).then_inc(S["y_p"], 1)
     zed(mate, False, False)
-    P.wait_ge(S["off_c"], got)
-    P.wait_ge(S["off_s"], got)
-    why(2, mine[0], 3).then_inc(S["y_dir"], 1)
-    for k in range(*mine):
-        zed(k, False, False)
-    P.wait_ge(S["fwd"], 2 * bits(near))
-    for i in range(3):
-        why(3 + i, theirs[0] + i, 1).then_inc(S["y_fwd%d" % i], 1)
-    for k in range(*theirs):
-        last = zed(k, False, k == theirs[1] - 1)
-    last.then_inc(S["z_all"], 1)
+    for n, (kind, k) in enumerate(seq):
+        if kind == "d":
+            P.wait_ge(S["dc%d" % k], nf)
+            P.wait_ge(S["dp%d" % k], nf)
+        else:
+            P.wait_ge(S["f%d" % k], 2 * bits(via[k]))
+        last = n == len(seq) - 1
+        if last:
+            zed(came(kind, k), False, True).then_inc(S["z_all"], 1)
+        why(2 + n, came(kind, k), 1).then_inc(S["y_%s%d" % (kind, k)], 1)
+        if not last:
+            zed(came(kind, k), False, False)
 
-    def act(bank, k, n, wait, done):
-        A.wait_ge(S[wait], 1)
-        A.activation(T.ysb[:, cols(k, n)], T["p%d" % bank][:, 0:n * L], ActivationFunctionType.Copy).then_inc(S[done], 1)
-
-    act(1, 0, 2, "y_pair", "c_pair")
-    act(2, mine[0], 3, "y_dir", "c_dir")
-    act(3, theirs[0], 1, "y_fwd0", "c_fwd0")
-    V.wait_ge(S["y_fwd1"], 1)
-    V.tensor_copy(T.ysb[:, cols(theirs[0] + 1)], T.p4[:, 0:L]).then_inc(S["c_fwd1"], 1)
-    act(5, theirs[0] + 2, 1, "y_fwd2", "c_fwd2")
+    A.wait_ge(S["y_p"], 1)
+    A.activation(T.ysb[:, cols(min(rank, mate), 2)], T.p1[:, 0:2 * L], ActivationFunctionType.Copy).then_inc(S["c_p"], 1)
+    for n, (kind, k) in enumerate(seq):
+        A.wait_ge(S["y_%s%d" % (kind, k)], 1)
+        A.activation(T.ysb[:, cols(came(kind, k))], T["p%d" % (2 + n)][:, 0:L], ActivationFunctionType.Copy).then_inc(S["c_%s%d" % (kind, k)], 1)
     V.wait_ge(S["z_all"], 1)
     V.tensor_copy(T.zsb[:], T.p0[:, 0:2 * L]).then_inc(S["c_z"], 1)
 
     stored = [0]
 
-    def store(lo, hi):
-        k = lo
-        while k < hi:
-            n = 1
-            while k + n < hi and rank_in(k + n) == rank_in(k) + n:
-                n += 1
-            Y.dma_start(T.y[:, cols(rank_in(k), n)], T.ysb[:, cols(k, n)]).then_inc(S["st"], 16)
-            stored[0] += 16
-            k += n
+    def store(queue, out, src):
+        queue.dma_start(out, src).then_inc(S["st"], 16)
+        stored[0] += 16
 
-    Y.wait_ge(S["c_pair"], 1)
-    store(0, 2)
-    Y.wait_ge(S["c_dir"], 1)
-    store(*mine)
-    for i in range(3):
-        Y.wait_ge(S["c_fwd%d" % i], 1)
-    store(*theirs)
-    A.wait_ge(S["c_z"], 1)
-    A.dma_start(T.z[:], T.zsb[:]).then_inc(S["st"], 16)
-    stored[0] += 16
+    Y.wait_ge(S["dp%d" % FAR[-1]], nf)
+    Y.wait_ge(S["c_p"], 1)
+    have = list(ranks[my])
+    for n, (kind, k) in enumerate(seq[:-1]):
+        Y.wait_ge(S["c_%s%d" % (kind, k)], 1)
+        have.append(came(kind, k))
+        if n in (0, 3, 4):
+            have.sort()
+            while have:
+                w = 1
+                while w < len(have) and have[w] == have[0] + w:
+                    w += 1
+                store(Y, T.y[:, cols(have[0], w)], T.ysb[:, cols(have[0], w)])
+                have = have[w:]
+    kind, k = seq[-1]
+    A.wait_ge(S["c_%s%d" % (kind, k)], 1)
+    store(A, T.y[:, cols(came(kind, k))], T.ysb[:, cols(came(kind, k))])
+    Y.wait_ge(S["c_z"], 1)
+    store(Y, T.z[:], T.zsb[:])
     Y.wait_ge(S["st"], stored[0])

from concourse.bass import DstId, RemoteDMATransfer
from concourse.mybir import dt, AluOpType, ActivationFunctionType

N = 8
G = 4
L = 128
C = 0.041
FAR = (1, 2, 3)
S_MASK = (0, 1)

SCRATCH = {
    "xb": ("sbuf", [128, 4 * L], "bfloat16"), "eb": ("sbuf", [128, 4 * L], "bfloat16"),
    "qxe": ("sbuf", [128, 2 * L], "float8_e4m3fn_x4"), "sxe": ("sbuf", [128, 2 * L], "uint8"),
    "ab": ("sbuf", [128, 16 * L], "bfloat16"), "qa": ("sbuf", [128, 4 * L], "float8_e4m3fn_x4"), "sa": ("sbuf", [128, 4 * L], "uint8"),
    "wb": ("sbuf", [128, 4 * L], "bfloat16"), "qw": ("sbuf", [128, L], "float8_e4m3fn_x4"), "sw": ("sbuf", [128, L], "uint8"),
    "vb": ("sbuf", [128, 8 * L], "bfloat16"), "qv": ("sbuf", [128, 2 * L], "float8_e4m3fn_x4"), "sv": ("sbuf", [128, 2 * L], "uint8"),
    "sg": ("sbuf", [128, 4 * L], "float32"), "m": ("sbuf", [128, 4 * L], "float32"), "t": ("sbuf", [128, 4 * L], "bfloat16"),
    "q": ("sbuf", [128, N * L], "float8_e4m3fn_x4"), "s": ("sbuf", [128, N * L], "uint8"),
    "ysb": ("sbuf", [128, N * L], "float32"), "zsb": ("sbuf", [128, 2 * L], "float32"),
}
for _k in range(8):
    SCRATCH["p%d" % _k] = ("psum", [128, 512], "float32")

SEMAPHORES = (["ld_x", "ld_e", "ld_w", "ld_v", "q_x", "q_e", "q_w", "q_v", "q_t", "peer", "sent", "z_all", "c_z", "y_p", "c_p", "st"]
              + ["%s%d" % (n, b) for n in ("ld_a", "q_a", "u", "d", "sg", "mk", "tt") for b in range(G)]
              + ["%s%d" % (n, k) for n in ("dc", "dp", "f", "y_d", "y_f", "c_d", "c_f") for k in FAR])


def bits(mask):
    return bin(mask).count("1")


def rank_program(g, core, T, topo):
    rank = T.rank_of(core)
    if rank is None:
        return
    S = T.sem
    V, P, A, Y = g.vector, g.tensor, g.scalar, g.sync

    chips = []
    for c in T.cores:
        if topo.chip(c) not in chips:
            chips.append(topo.chip(c))
    ranks = [[r for r, c in enumerate(T.cores) if topo.chip(c) == ch] for ch in chips]
    my = chips.index(topo.chip(core))
    i = ranks[my].index(rank)
    mate = ranks[my][1 - i]
    peer = T.cores[mate]

    def came(kind, k):
        return ranks[(my - k) % len(chips)][i if kind == "d" else 1 - i]

    def cols(k, n=1, w=L):
        return slice(k * w, (k + n) * w)

    def codes(k):
        return T.q[:, cols(k)].bitcast(dt.uint8)

    def plane(k):
        return T.s[:, cols(k)]

    def load_a(b, queue):
        queue.dma_start(T.ab[:, cols(b, 1, 4 * L)], T.a[:, cols(b, 1, 4 * L)]).then_inc(S["ld_a%d" % b], 16)

    Y.dma_start(T.xb[:], T.x[:]).then_inc(S["ld_x"], 16)
    load_a(0, A)
    Y.dma_start(T.eb[:], T.e[:]).then_inc(S["ld_e"], 16)
    for b in (1, 2, 3):
        load_a(b, Y)
    Y.wait_ge(S["ld_x"], 16)
    Y.wait_ge(S["ld_e"], 16)
    Y.dma_start(T.vb[:], T.v[:]).then_inc(S["ld_v"], 16)
    Y.dma_start(T.wb[:], T.w[:]).then_inc(S["ld_w"], 16)

    def q_in(k):
        nm = "xe"[k]
        V.wait_ge(S["ld_" + nm], 16)
        V.quantize_mx(T.qxe[:, cols(k)], T.sxe[:, cols(k)], T[nm + "b"][:]).then_inc(S["q_" + nm], 1)

    def q_a(b):
        V.wait_ge(S["ld_a%d" % b], 16)
        V.quantize_mx(T.qa[:, cols(b)], T.sa[:, cols(b)], T.ab[:, cols(b, 1, 4 * L)]).then_inc(S["q_a%d" % b], 1)

    def mask(b):
        V.wait_ge(S["u%d" % b], 1)
        V.tensor_scalar(T.m[:, cols(b)], T["p%d" % b][:, 0:L], 0.0, C, AluOpType.is_gt, AluOpType.mult).then_inc(S["mk%d" % b], 1)

    def piece(b):
        V.wait_ge(S["d%d" % b], 1)
        V.wait_ge(S["mk%d" % b], 1)
        V.tensor_tensor(T.t[:, b:4 * L:4], T["p%d" % (4 + b)][:, 0:L], T.m[:, cols(b)], AluOpType.mult).then_inc(S["tt%d" % b], 1)

    for call, b in ((q_in, 0), (q_a, 0), (q_in, 1), (q_a, 1), (piece, 0), (q_a, 2), (q_a, 3), (piece, 1),
                    (mask, 2), (mask, 3), (piece, 2), (piece, 3)):
        call(b)
    for b in range(G):
        V.wait_ge(S["tt%d" % b], 1)
    V.quantize_mx(T.q[:, cols(rank)], T.s[:, cols(rank)], T.t[:]).then_inc(S["q_t"], 1)
    V.wait_ge(S["ld_v"], 16)
    V.quantize_mx(T.qv[:], T.sv[:], T.vb[:]).then_inc(S["q_v"], 1)
    V.wait_ge(S["ld_w"], 16)
    V.quantize_mx(T.qw[:], T.sw[:], T.wb[:]).then_inc(S["q_w"], 1)

    for b in S_MASK:
        A.wait_ge(S["u%d" % b], 1)
        A.activation(T.sg[:, cols(b)], T["p%d" % b][:, 0:L], ActivationFunctionType.Sign).then_inc(S["sg%d" % b], 1)
        A.wait_ge(S["sg%d" % b], 1)
        A.activation(T.m[:, cols(b)], T.sg[:, cols(b)], ActivationFunctionType.Relu, scale=C).then_inc(S["mk%d" % b], 1)

    for b in range(G):
        for k in range(2):
            P.wait_ge(S["q_" + "xe"[k]], 1)
            P.wait_ge(S["q_a%d" % b], 1)
            P.matmul_mx(T["p%d" % (4 * k + b)][:, 0:L], T.qa[:, cols(b)], T.sa[:, cols(b)],
                        T.qxe[:, cols(k)], T.sxe[:, cols(k)], True, True).then_inc(S["%s%d" % ("ud"[k], b)], 1)

    to = {k: T.cores[ranks[(my + k) % len(chips)][i]] for k in FAR}
    near = topo.mask(core, peer)
    far = near
    for k in FAR:
        far &= topo.mask(core, to[k])
    side = near & ~far
    nf, ns = bits(far), bits(side)
    sent = [0]

    def part(dst, view, slot, mask, sem):
        rid, pid, _ = topo.addr(dst)
        sent[0] += bits(mask)
        return RemoteDMATransfer(dst_ids=[DstId(rid=rid, pnc=pid)], dma_engine_mask=mask, remote_sem=S[sem],
                                 src=view(slot), dsts=[view(slot)])

    both = (("dc", codes), ("dp", plane))
    g.wait_ge(S["q_t"], 1)
    for k in FAR:
        for sem, view in both:
            parts = [part(to[k], view, rank, far, "%s%d" % (sem, k))]
            if k == FAR[1]:
                parts.append(part(peer, view, rank, side, "peer"))
            g.remote_dma_fused(parts, local_sem=S["sent"])
    via = {k: side for k in FAR}
    via[FAR[-1]] = near
    for k in FAR:
        for sem, view in both:
            g.wait_ge(S["%s%d" % (sem, k)], nf)
            g.remote_dma_fused([part(peer, view, came("d", k), via[k], "f%d" % k)], local_sem=S["sent"])
    g.wait_ge(S["sent"], sent[0])

    seq = [("d", FAR[0]), ("d", FAR[1]), ("f", FAR[0]), ("d", FAR[2]), ("f", FAR[1]), ("f", FAR[2])]

    def zed(k, start, stop):
        return P.matmul_mx(T.p0[:, 0:2 * L], T.q[:, cols(k)], T.s[:, cols(k)], T.qv[:], T.sv[:], start, stop)

    def why(bank, k, n):
        return P.matmul_mx(T["p%d" % bank][:, 0:n * L], T.qw[:], T.sw[:], T.q[:, cols(k, n)], T.s[:, cols(k, n)], True, True)

    P.wait_ge(S["q_t"], 1)
    P.wait_ge(S["q_v"], 1)
    zed(rank, True, False)
    P.wait_ge(S["q_w"], 1)
    P.wait_ge(S["peer"], 2 * ns)
    why(1, min(rank, mate), 2).then_inc(S["y_p"], 1)
    zed(mate, False, False)
    for n, (kind, k) in enumerate(seq):
        if kind == "d":
            P.wait_ge(S["dc%d" % k], nf)
            P.wait_ge(S["dp%d" % k], nf)
        else:
            P.wait_ge(S["f%d" % k], 2 * bits(via[k]))
        last = n == len(seq) - 1
        if last:
            zed(came(kind, k), False, True).then_inc(S["z_all"], 1)
        why(2 + n, came(kind, k), 1).then_inc(S["y_%s%d" % (kind, k)], 1)
        if not last:
            zed(came(kind, k), False, False)

    A.wait_ge(S["y_p"], 1)
    A.activation(T.ysb[:, cols(min(rank, mate), 2)], T.p1[:, 0:2 * L], ActivationFunctionType.Copy).then_inc(S["c_p"], 1)
    for n, (kind, k) in enumerate(seq):
        A.wait_ge(S["y_%s%d" % (kind, k)], 1)
        A.activation(T.ysb[:, cols(came(kind, k))], T["p%d" % (2 + n)][:, 0:L], ActivationFunctionType.Copy).then_inc(S["c_%s%d" % (kind, k)], 1)
    V.wait_ge(S["z_all"], 1)
    V.tensor_copy(T.zsb[:], T.p0[:, 0:2 * L]).then_inc(S["c_z"], 1)

    stored = [0]

    def store(queue, out, src):
        queue.dma_start(out, src).then_inc(S["st"], 16)
        stored[0] += 16

    Y.wait_ge(S["dp%d" % FAR[-1]], nf)
    Y.wait_ge(S["c_p"], 1)
    have = list(ranks[my])
    for n, (kind, k) in enumerate(seq[:-1]):
        Y.wait_ge(S["c_%s%d" % (kind, k)], 1)
        have.append(came(kind, k))
        if n in (0, 3, 4):
            have.sort()
            while have:
                w = 1
                while w < len(have) and have[w] == have[0] + w:
                    w += 1
                store(Y, T.y[:, cols(have[0], w)], T.ysb[:, cols(have[0], w)])
                have = have[w:]
    kind, k = seq[-1]
    A.wait_ge(S["c_%s%d" % (kind, k)], 1)
    store(A, T.y[:, cols(came(kind, k))], T.ysb[:, cols(came(kind, k))])
    Y.wait_ge(S["c_z"], 1)
    store(Y, T.z[:], T.zsb[:])
    Y.wait_ge(S["st"], stored[0])
